import numpy as np
import ml_dtypes


def mxq(x, axis, fmt="e4m3"):
    dtype, down = {"e4m3": (ml_dtypes.float8_e4m3fn, 7), "e5m2": (ml_dtypes.float8_e5m2, 14)}[fmt]
    v = np.moveaxis(np.asarray(x, np.float32).astype(ml_dtypes.bfloat16).astype(np.float64), axis, -1)
    blocks = v.reshape(v.shape[:-1] + (-1, 32))
    amax = np.abs(blocks).max(-1, keepdims=True)
    byte = np.maximum(np.where(amax > 0, np.frexp(amax)[1] - 1 + 127, 0) - down, 1)
    scale = np.exp2(byte - 127.0)
    codes = (blocks / scale).astype(np.float32).astype(dtype).astype(np.float64)
    return np.moveaxis((codes * scale).reshape(v.shape), -1, axis)


WIDE = False


def mx_kscale(k):
    if not WIDE:
        return np.ones(k)
    levels = np.array([10, -10, 5, -5, 0])
    if k % 512:
        return np.exp2(np.random.permutation(np.resize(levels, k // 32))).repeat(32)
    a = np.empty((k // 512, 16))
    for p in range(k // 512):
        a[p, :8] = np.random.permutation(np.resize(levels, 8))
        for g in range(8):
            far = levels[np.abs(levels - a[p, g]) >= 10]
            a[p, g + 8] = far[np.random.randint(len(far))]
    return np.exp2(a.ravel()).repeat(32)


def f64(x):
    return np.asarray(x).astype(np.float64)


def striped(idx):
    return np.tile(idx.reshape(-1, 16).T, (8, 1)).astype(np.uint16)


def unstriped(offs):
    return offs[:16].T.reshape(-1).astype(np.int64)


def silu(v):
    return v / (1.0 + np.exp(-np.maximum(v, -700.0)))


K, T, D, S, V, N = 1024, 1024, 2, 1024, 512, 512


def setup_inputs():
    n = np.random.standard_normal
    s = mx_kscale(K)[:, None]
    return {
        "xT": (n((K, T)) * s / np.sqrt(D)).astype(ml_dtypes.bfloat16).astype(np.float32),
        "w": (n((K, N)) / np.sqrt(K) / s).astype(np.float32),
        "b": (0.3 * n((N, 1))).astype(np.float32),
        "offs": striped(np.concatenate([np.random.permutation(T)[:V] for _ in range(D)])),
    }


def reference(xT, w, b, offs):
    idx = unstriped(offs)
    x = sum(f64(xT)[:, idx[d * V:(d + 1) * V]] for d in range(D))
    return silu((mxq(f64(w), 0, "e4m3").T @ mxq(x, 0, "e4m3")) + f64(b))

@@ -1,0 +1,203 @@
+from contextlib import ExitStack
+
+import concourse.mybir as mybir
+
+K, T, D, V, N = 1024, 1024, 2, 512, 512
+FLOPS = 2 * K * V * N
+
+F32 = mybir.dt.float32
+BF16 = mybir.dt.bfloat16
+U32 = mybir.dt.uint32
+U16 = mybir.dt.uint16
+U8 = mybir.dt.uint8
+FP8X4 = mybir.dt.float8_e4m3fn_x4
+SILU = mybir.ActivationFunctionType.Silu
+ADD = mybir.AluOpType.add
+MULT = mybir.AluOpType.mult
+
+P = 128
+PASSES = 2
+BLOCKS = N // P
+PIECES = ((0, 256), (256, 384), (384, 512))
+
+
+def tile_picked_hash_lin_silu_sub_l_kernel(tc, xT, w, b, offs, out):
+    nc = tc.nc
+    x_rows = xT.rearrange("(g p u e) t -> g u p e t", g=PASSES, p=P, u=2, e=2)
+    w_rows = w.rearrange("(g p j) m -> g p j m", g=PASSES, p=P, j=4)
+    out_rows = out.rearrange("(c p) v -> p c v", p=P)
+
+    with ExitStack() as ctx:
+        keep = ctx.enter_context(tc.tile_pool(name="keep", bufs=1))
+        psum = ctx.enter_context(tc.psum_pool(name="psum", bufs=1))
+
+        offsets = keep.tile([P, D * V // 16], U16, name="offsets")
+        bias = keep.tile([P, BLOCKS], F32, name="bias")
+        table = [[keep.tile([P, 2, T], F32, name=f"table{g}{u}", align_bytes=64) for u in range(2)] for g in range(PASSES)]
+        w_raw = [[keep.tile([P, 4, N // WSPLIT[g]], F32, name=f"w_raw{g}{h}", align_bytes=64) for h in range(WSPLIT[g])] for g in range(PASSES)]
+        shared = keep.tile([P, V + 256 + 1024], F32, name="shared", align_bytes=64)
+        w_bf = [keep.tile([P, N, 4], BF16, name=f"w_bf{g}", align_bytes=64) for g in range(PASSES)]
+        w_codes = [keep.tile([P, N], U32, name=f"w_codes{g}", align_bytes=64) for g in range(PASSES)]
+        w_scales = [keep.tile([P, N], U8, name=f"w_scales{g}", align_bytes=64) for g in range(PASSES)]
+        picked = [[keep.tile([P, 2, V, 2], BF16, name=f"picked{g}{d}", align_bytes=64) for d in range(D)] for g in range(PASSES)]
+        picked[1][1] = shared[:, 0:2 * V].bitcast(BF16).rearrange("p (u v e) -> p u v e", u=2, e=2)
+        w_raw[1][1] = shared[:, V + 256:].rearrange("p (j m) -> p j m", j=4)
+        x_bf = [keep.tile([P, V, 4], BF16, name=f"x_bf{g}", align_bytes=64) for g in range(PASSES)]
+        x_codes = [keep.tile([P, V], U32, name=f"x_codes{g}", align_bytes=64) for g in range(PASSES)]
+        x_scales = [keep.tile([P, V], U8, name=f"x_scales{g}", align_bytes=64) for g in range(PASSES)]
+        banks = [psum.tile([P, 512], F32, name=f"bank{i}") for i in range(8)]
+        result = [keep.tile([P, BLOCKS, hi - lo], F32, name=f"result{i}") for i, (lo, hi) in enumerate(PIECES)]
+        warm = keep.tile([P, 2], F32, name="warm")
+
+        def load_x(g, u, lo, hi):
+            nc.sync.dma_start(out=table[g][u][:, :, lo:hi], in_=x_rows[g, u, :, :, lo:hi])
+
+        def load_w(g, h):
+            n = N // WSPLIT[g]
+            nc.sync.dma_start(out=w_raw[g][h][:, :, :], in_=w_rows[g, :, :, h * n:(h + 1) * n])
+
+        def pack(g, u, lo, hi, on_vector=False):
+            halves = table[g][u][:, 1, :].bitcast(BF16).rearrange("p (t e) -> p t e", e=2)
+            if on_vector:
+                nc.vector.tensor_copy(out=halves[:, lo:hi, 0], in_=table[g][u][:, 0, lo:hi])
+            else:
+                nc.scalar.copy(out=halves[:, lo:hi, 0], in_=table[g][u][:, 0, lo:hi])
+
+        def weave_w(g, lo, hi, on_pool=False):
+            n = N // WSPLIT[g]
+            h = lo // n
+            dst = w_bf[g][:, lo:hi, :].rearrange("p (c i) j -> p c j i", i=4)
+            src = w_raw[g][h][:, :, lo - h * n:hi - h * n].rearrange("p j (c i) -> p c j i", i=4)
+            if on_pool:
+                nc.gpsimd.tensor_scalar(out=dst, in0=src, scalar1=1.0, scalar2=0.0, op0=MULT, op1=ADD)
+            else:
+                nc.scalar.copy(out=dst, in_=src)
+
+        def quantise(codes, scales, grouped, lo, hi):
+            nc.vector.quantize_mx(
+                out=codes[:, lo:hi].bitcast(FP8X4),
+                scales=scales[:, lo:hi],
+                in_=grouped[:, lo:hi, :].rearrange("p n j -> p (n j)"),
+            )
+
+        def gather(g, u, d, lo, hi):
+            window = table[g][u][:, 1, :].bitcast(U32)
+            words = picked[g][d][:, u, lo:hi, :].rearrange("p v e -> p (v e)").bitcast(U32)
+            nc.vector.tensor_copy(words, window.indirect(offsets[:, (d * V + lo) // 16:(d * V + hi) // 16]))
+
+        def add(g, lo, hi, engine=nc.vector):
+            engine.tensor_tensor(
+                out=x_bf[g][:, lo:hi, :].rearrange("p v (u e) -> p v u e", e=2),
+                in0=picked[g][0][:, :, lo:hi, :].rearrange("p u v e -> p v u e"),
+                in1=picked[g][1][:, :, lo:hi, :].rearrange("p u v e -> p v u e"),
+                op=ADD,
+            )
+
+        def acc(i, c):
+            lo, hi = PIECES[i]
+            if i == len(PIECES) - 1:
+                return banks[BLOCKS + c][:, 0:hi - lo]
+            return banks[c][:, lo:hi]
+
+        def multiply(i, c, g):
+            lo, hi = PIECES[i]
+            cols = slice(c * P, (c + 1) * P)
+            nc.tensor.matmul_mx(
+                out=acc(i, c),
+                lhsT=w_codes[g][:, cols].bitcast(FP8X4),
+                lhsT_scale=w_scales[g][:, cols],
+                rhs=x_codes[g][:, lo:hi].bitcast(FP8X4),
+                rhs_scale=x_scales[g][:, lo:hi],
+                start=(g == 0),
+                stop=(g == PASSES - 1),
+            )
+
+        def finish(i, c):
+            nc.scalar.activation(out=result[i][:, c, :], in_=acc(i, c), func=SILU, bias=bias[:, c:c + 1])
+
+        def store(i, c0, c1, queue):
+            lo, hi = PIECES[i]
+            queue.dma_start(out=out_rows[:, c0:c1, lo:hi], in_=result[i][:, c0:c1, :])
+
+        nc.vector.memset(warm[:, 0:1], 0.0)
+        nc.scalar.activation(out=warm[:, 1:2], in_=warm[:, 0:1], func=SILU)
+
+        load_x(0, 0, 0, 512)
+        nc.sync.dma_start(offsets[:], offs)
+        load_x(0, 0, 512, 1024)
+        load_x(0, 1, 0, 512)
+        load_x(0, 1, 512, 1024)
+        load_w(0, 0)
+        load_w(0, 1)
+        load_x(1, 0, 0, 512)
+        load_x(1, 0, 512, 1024)
+        load_x(1, 1, 0, 512)
+        load_x(1, 1, 512, 1024)
+        load_w(1, 0)
+        load_w(1, 1)
+        with nc.allow_non_contiguous_dma(reason="one bias value a partition and block"):
+            nc.sync.dma_start(out=bias[:], in_=b.rearrange("(c p) o -> p (c o)", p=P))
+
+        pack(0, 0, 0, 512)
+        pack(0, 0, 512, 896, on_vector=True)
+        pack(0, 0, 896, 1024)
+        gather(0, 0, 0, 0, V)
+        gather(0, 0, 1, 0, V)
+        pack(0, 1, 0, 512)
+        pack(0, 1, 512, 1024)
+        gather(0, 1, 0, 0, V)
+        gather(0, 1, 1, 0, 256)
+        gather(0, 1, 1, 256, V)
+        weave_w(0, 0, 256)
+        weave_w(0, 256, 512)
+        add(0, 0, 256)
+        add(0, 256, V)
+        quantise(x_codes[0], x_scales[0], x_bf[0], 0, 256)
+        quantise(x_codes[0], x_scales[0], x_bf[0], 256, V)
+        quantise(w_codes[0], w_scales[0], w_bf[0], 0, 256)
+        quantise(w_codes[0], w_scales[0], w_bf[0], 256, 512)
+        pack(1, 0, 0, 512)
+        pack(1, 0, 512, 1024)
+        gather(1, 0, 0, 0, V)
+        gather(1, 0, 1, 0, V)
+        for c in range(BLOCKS):
+            multiply(0, c, 0)
+            multiply(2, c, 0)
+        pack(1, 1, 0, 512)
+        pack(1, 1, 512, 1024)
+        weave_w(1, 0, 256)
+        weave_w(1, 256, 512)
+        a, m, z = PIECES
+        gather(1, 1, 0, *a)
+        gather(1, 1, 1, *a)
+        gather(1, 1, 0, *m)
+        add(1, *a)
+        gather(1, 1, 0, *z)
+        quantise(x_codes[1], x_scales[1], x_bf[1], *a)
+        quantise(w_codes[1], w_scales[1], w_bf[1], 0, 256)
+        quantise(w_codes[1], w_scales[1], w_bf[1], 256, 512)
+        for c in range(BLOCKS):
+            multiply(0, c, 1)
+            finish(0, c)
+        store(0, 0, BLOCKS, nc.sync)
+        for c in range(BLOCKS):
+            multiply(1, c, 0)
+        gather(1, 1, 1, *m)
+        gather(1, 1, 1, *z)
+        add(1, *m)
+        add(1, *z)
+        quantise(x_codes[1], x_scales[1], x_bf[1], *m)
+        quantise(x_codes[1], x_scales[1], x_bf[1], *z)
+        for c in range(BLOCKS):
+            multiply(1, c, 1)
+            finish(1, c)
+        store(1, 0, BLOCKS, nc.sync)
+        for c in range(BLOCKS):
+            multiply(2, c, 1)
+            finish(2, c)
+            if c == 1:
+                store(2, 0, 2, nc.sync)
+        store(2, 2, 4, nc.sync)
+
+
+WSPLIT = (2, 2)

@@ -18,6 +18,7 @@ MULT = mybir.AluOpType.mult
 P = 128
 PASSES = 2
 BLOCKS = N // P
+HALF = V // 2
 PIECES = ((0, 256), (256, 384), (384, 512))
 
 
@@ -34,62 +35,82 @@ def tile_picked_hash_lin_silu_sub_l_kernel(tc, xT, w, b, offs, out):
         offsets = keep.tile([P, D * V // 16], U16, name="offsets")
         bias = keep.tile([P, BLOCKS], F32, name="bias")
         table = [[keep.tile([P, 2, T], F32, name=f"table{g}{u}", align_bytes=64) for u in range(2)] for g in range(PASSES)]
-        w_raw = [[keep.tile([P, 4, N // WSPLIT[g]], F32, name=f"w_raw{g}{h}", align_bytes=64) for h in range(WSPLIT[g])] for g in range(PASSES)]
-        shared = keep.tile([P, V + 256 + 1024], F32, name="shared", align_bytes=64)
-        w_bf = [keep.tile([P, N, 4], BF16, name=f"w_bf{g}", align_bytes=64) for g in range(PASSES)]
+        picked0 = keep.tile([P, 4 * V + HALF], F32, name="picked0", align_bytes=64)
+        picked1 = keep.tile([P, 3 * V + 4 * N], F32, name="picked1", align_bytes=64)
+        w_raw0 = keep.tile([P, 4 * N], F32, name="w_raw0", align_bytes=64)
+        w_raw = [w_raw0[:, :].rearrange("p (j m) -> p j m", j=4), picked1[:, 3 * V:].rearrange("p (j m) -> p j m", j=4)]
+        w_bf = [[keep.tile([P, N // 2, 4], BF16, name=f"w_bf{g}{h}", tag=f"w_bf{g}{h}", align_bytes=64) for h in range(2)] for g in range(PASSES)]
         w_codes = [keep.tile([P, N], U32, name=f"w_codes{g}", align_bytes=64) for g in range(PASSES)]
         w_scales = [keep.tile([P, N], U8, name=f"w_scales{g}", align_bytes=64) for g in range(PASSES)]
-        picked = [[keep.tile([P, 2, V, 2], BF16, name=f"picked{g}{d}", align_bytes=64) for d in range(D)] for g in range(PASSES)]
-        picked[1][1] = shared[:, 0:2 * V].bitcast(BF16).rearrange("p (u v e) -> p u v e", u=2, e=2)
-        w_raw[1][1] = shared[:, V + 256:].rearrange("p (j m) -> p j m", j=4)
-        x_bf = [keep.tile([P, V, 4], BF16, name=f"x_bf{g}", align_bytes=64) for g in range(PASSES)]
+        x_bf = [keep.tile([P, 4 * V], BF16, name=f"x_bf{g}", align_bytes=64) for g in range(PASSES)]
         x_codes = [keep.tile([P, V], U32, name=f"x_codes{g}", align_bytes=64) for g in range(PASSES)]
         x_scales = [keep.tile([P, V], U8, name=f"x_scales{g}", align_bytes=64) for g in range(PASSES)]
         banks = [psum.tile([P, 512], F32, name=f"bank{i}") for i in range(8)]
         result = [keep.tile([P, BLOCKS, hi - lo], F32, name=f"result{i}") for i, (lo, hi) in enumerate(PIECES)]
         warm = keep.tile([P, 2], F32, name="warm")
 
-        def load_x(g, u, lo, hi):
-            nc.sync.dma_start(out=table[g][u][:, :, lo:hi], in_=x_rows[g, u, :, :, lo:hi])
+        def place(g, u, d, v):
+            if g == 0:
+                return (2 * d + u) * V + v
+            if u == 0:
+                return d * V + v
+            if v < HALF:
+                return 2 * V + d * HALF + v
+            return 3 * V + d * HALF + v - HALF
 
-        def load_w(g, h):
-            n = N // WSPLIT[g]
-            nc.sync.dma_start(out=w_raw[g][h][:, :, :], in_=w_rows[g, :, :, h * n:(h + 1) * n])
+        def sums(g, lo, hi):
+            if g == 1 and hi <= HALF:
+                return w_raw0[:, 2 * lo:2 * hi].bitcast(BF16)
+            return x_bf[g][:, 4 * lo:4 * hi]
 
-        def pack(g, u, lo, hi, on_vector=False):
+        late_codes = []
+
+        def codes(g, lo, hi):
+            if g == 0 and lo >= HALF:
+                return late_codes[0][:, lo - HALF:hi - HALF].bitcast(FP8X4)
+            return x_codes[g][:, lo:hi].bitcast(FP8X4)
+
+        def pack(g, u, lo, hi, engine):
             halves = table[g][u][:, 1, :].bitcast(BF16).rearrange("p (t e) -> p t e", e=2)
-            if on_vector:
+            if engine == "v":
                 nc.vector.tensor_copy(out=halves[:, lo:hi, 0], in_=table[g][u][:, 0, lo:hi])
+            elif engine == "g":
+                nc.gpsimd.tensor_copy(out=halves[:, lo:hi, 0], in_=table[g][u][:, 0, lo:hi])
             else:
                 nc.scalar.copy(out=halves[:, lo:hi, 0], in_=table[g][u][:, 0, lo:hi])
 
-        def weave_w(g, lo, hi, on_pool=False):
-            n = N // WSPLIT[g]
-            h = lo // n
-            dst = w_bf[g][:, lo:hi, :].rearrange("p (c i) j -> p c j i", i=4)
-            src = w_raw[g][h][:, :, lo - h * n:hi - h * n].rearrange("p j (c i) -> p c j i", i=4)
-            if on_pool:
-                nc.gpsimd.tensor_scalar(out=dst, in0=src, scalar1=1.0, scalar2=0.0, op0=MULT, op1=ADD)
-            else:
-                nc.scalar.copy(out=dst, in_=src)
+        def weave_w(g, lo, hi):
+            dst = w_bf[g][lo // 256][:, :, :].rearrange("p (c i) j -> p c j i", i=4)
+            src = w_raw[g][:, :, lo:hi].rearrange("p j (c i) -> p c j i", i=4)
+            nc.scalar.copy(out=dst, in_=src)
 
-        def quantise(codes, scales, grouped, lo, hi):
+        def quantise_w(g, lo, hi):
             nc.vector.quantize_mx(
-                out=codes[:, lo:hi].bitcast(FP8X4),
-                scales=scales[:, lo:hi],
-                in_=grouped[:, lo:hi, :].rearrange("p n j -> p (n j)"),
+                out=w_codes[g][:, lo:hi].bitcast(FP8X4),
+                scales=w_scales[g][:, lo:hi],
+                in_=w_bf[g][lo // 256][:, :, :].rearrange("p n j -> p (n j)"),
             )
+
+        def quantise_x(g, lo, hi):
+            nc.vector.quantize_mx(out=codes(g, lo, hi), scales=x_scales[g][:, lo:hi], in_=sums(g, lo, hi))
 
         def gather(g, u, d, lo, hi):
             window = table[g][u][:, 1, :].bitcast(U32)
-            words = picked[g][d][:, u, lo:hi, :].rearrange("p v e -> p (v e)").bitcast(U32)
+            first = place(g, u, d, lo)
+            words = (picked0, picked1)[g][:, first:first + hi - lo].bitcast(U32)
             nc.vector.tensor_copy(words, window.indirect(offsets[:, (d * V + lo) // 16:(d * V + hi) // 16]))
+
+        def pairs(g, d, lo, hi):
+            first = place(g, 0, d, lo)
+            step = place(g, 1, d, lo) - first
+            both = (picked0, picked1)[g][:, first:first + 2 * step].bitcast(BF16).rearrange("p (u v e) -> p v u e", u=2, e=2)
+            return both[:, 0:hi - lo, :, :]
 
         def add(g, lo, hi, engine=nc.vector):
             engine.tensor_tensor(
-                out=x_bf[g][:, lo:hi, :].rearrange("p v (u e) -> p v u e", e=2),
-                in0=picked[g][0][:, :, lo:hi, :].rearrange("p u v e -> p v u e"),
-                in1=picked[g][1][:, :, lo:hi, :].rearrange("p u v e -> p v u e"),
+                out=sums(g, lo, hi).rearrange("p (v u e) -> p v u e", u=2, e=2),
+                in0=pairs(g, 0, lo, hi),
+                in1=pairs(g, 1, lo, hi),
                 op=ADD,
             )
 
@@ -106,7 +127,7 @@ def tile_picked_hash_lin_silu_sub_l_kernel(tc, xT, w, b, offs, out):
                 out=acc(i, c),
                 lhsT=w_codes[g][:, cols].bitcast(FP8X4),
                 lhsT_scale=w_scales[g][:, cols],
-                rhs=x_codes[g][:, lo:hi].bitcast(FP8X4),
+                rhs=codes(g, lo, hi),
                 rhs_scale=x_scales[g][:, lo:hi],
                 start=(g == 0),
                 stop=(g == PASSES - 1),
@@ -122,72 +143,66 @@ def tile_picked_hash_lin_silu_sub_l_kernel(tc, xT, w, b, offs, out):
         nc.vector.memset(warm[:, 0:1], 0.0)
         nc.scalar.activation(out=warm[:, 1:2], in_=warm[:, 0:1], func=SILU)
 
-        load_x(0, 0, 0, 512)
+        nc.sync.dma_start(out=table[0][0][:], in_=x_rows[0, 0])
         nc.sync.dma_start(offsets[:], offs)
-        load_x(0, 0, 512, 1024)
-        load_x(0, 1, 0, 512)
-        load_x(0, 1, 512, 1024)
-        load_w(0, 0)
-        load_w(0, 1)
-        load_x(1, 0, 0, 512)
-        load_x(1, 0, 512, 1024)
-        load_x(1, 1, 0, 512)
-        load_x(1, 1, 512, 1024)
-        load_w(1, 0)
-        load_w(1, 1)
+        nc.sync.dma_start(out=table[0][1][:], in_=x_rows[0, 1])
+        nc.sync.dma_start(out=table[1][0][:], in_=x_rows[1, 0])
+        nc.sync.dma_start(out=table[1][1][:], in_=x_rows[1, 1])
+        nc.sync.dma_start(out=w_raw[0], in_=w_rows[0])
+        nc.sync.dma_start(out=w_raw[1], in_=w_rows[1])
         with nc.allow_non_contiguous_dma(reason="one bias value a partition and block"):
             nc.sync.dma_start(out=bias[:], in_=b.rearrange("(c p) o -> p (c o)", p=P))
 
-        pack(0, 0, 0, 512)
-        pack(0, 0, 512, 896, on_vector=True)
-        pack(0, 0, 896, 1024)
+        pack(0, 0, 0, 688, "v")
+        pack(0, 0, 688, T, "s")
         gather(0, 0, 0, 0, V)
         gather(0, 0, 1, 0, V)
-        pack(0, 1, 0, 512)
-        pack(0, 1, 512, 1024)
+        pack(0, 1, 0, 400, "v")
+        pack(0, 1, 400, T, "s")
         gather(0, 1, 0, 0, V)
-        gather(0, 1, 1, 0, 256)
-        gather(0, 1, 1, 256, V)
-        weave_w(0, 0, 256)
-        weave_w(0, 256, 512)
-        add(0, 0, 256)
-        add(0, 256, V)
-        quantise(x_codes[0], x_scales[0], x_bf[0], 0, 256)
-        quantise(x_codes[0], x_scales[0], x_bf[0], 256, V)
-        quantise(w_codes[0], w_scales[0], w_bf[0], 0, 256)
-        quantise(w_codes[0], w_scales[0], w_bf[0], 256, 512)
-        pack(1, 0, 0, 512)
-        pack(1, 0, 512, 1024)
+        gather(0, 1, 1, 0, HALF)
+        gather(0, 1, 1, HALF, V)
+        add(0, 0, HALF)
+        add(0, HALF, V)
+        quantise_x(0, 0, HALF)
+        pack(1, 0, 0, T, "s")
         gather(1, 0, 0, 0, V)
         gather(1, 0, 1, 0, V)
-        for c in range(BLOCKS):
-            multiply(0, c, 0)
-            multiply(2, c, 0)
-        pack(1, 1, 0, 512)
-        pack(1, 1, 512, 1024)
+        pack(1, 1, 0, T, "s")
+        weave_w(0, 0, 256)
+        weave_w(0, 256, 512)
         weave_w(1, 0, 256)
         weave_w(1, 256, 512)
         a, m, z = PIECES
         gather(1, 1, 0, *a)
         gather(1, 1, 1, *a)
-        gather(1, 1, 0, *m)
+        quantise_w(0, 0, 256)
         add(1, *a)
+        quantise_w(0, 256, 512)
+        quantise_x(1, *a)
+        for c in range(BLOCKS):
+            multiply(0, c, 0)
+        quantise_w(1, 0, 256)
+        gather(1, 1, 0, *m)
+        late_codes.append(keep.tile([P, HALF], U32, name="late_codes", tag="w_bf10", align_bytes=64))
+        quantise_x(0, HALF, V)
         gather(1, 1, 0, *z)
-        quantise(x_codes[1], x_scales[1], x_bf[1], *a)
-        quantise(w_codes[1], w_scales[1], w_bf[1], 0, 256)
-        quantise(w_codes[1], w_scales[1], w_bf[1], 256, 512)
+        quantise_w(1, 256, 512)
         for c in range(BLOCKS):
             multiply(0, c, 1)
             finish(0, c)
-        store(0, 0, BLOCKS, nc.sync)
+            if c % 2 == 1:
+                store(0, c - 1, c + 1, nc.sync)
+        for c in range(BLOCKS):
+            multiply(2, c, 0)
         for c in range(BLOCKS):
             multiply(1, c, 0)
         gather(1, 1, 1, *m)
         gather(1, 1, 1, *z)
         add(1, *m)
         add(1, *z)
-        quantise(x_codes[1], x_scales[1], x_bf[1], *m)
-        quantise(x_codes[1], x_scales[1], x_bf[1], *z)
+        quantise_x(1, *m)
+        quantise_x(1, *z)
         for c in range(BLOCKS):
             multiply(1, c, 1)
             finish(1, c)
@@ -197,7 +212,6 @@ def tile_picked_hash_lin_silu_sub_l_kernel(tc, xT, w, b, offs, out):
             finish(2, c)
             if c == 1:
                 store(2, 0, 2, nc.sync)
-        store(2, 2, 4, nc.sync)
-
-
-WSPLIT = (2, 2)
+            if c == 2:
+                store(2, 2, 3, nc.sync)
+        store(2, 3, 4, nc.scalar)

@@ -35,15 +35,14 @@ def tile_picked_hash_lin_silu_sub_l_kernel(tc, xT, w, b, offs, out):
         offsets = keep.tile([P, D * V // 16], U16, name="offsets")
         bias = keep.tile([P, BLOCKS], F32, name="bias")
         table = [[keep.tile([P, 2, T], F32, name=f"table{g}{u}", align_bytes=64) for u in range(2)] for g in range(PASSES)]
-        picked0 = keep.tile([P, 4 * V + HALF], F32, name="picked0", align_bytes=64)
-        picked1 = keep.tile([P, 3 * V + 4 * N], F32, name="picked1", align_bytes=64)
-        w_raw0 = keep.tile([P, 4 * N], F32, name="w_raw0", align_bytes=64)
-        w_raw = [w_raw0[:, :].rearrange("p (j m) -> p j m", j=4), picked1[:, 3 * V:].rearrange("p (j m) -> p j m", j=4)]
+        picked0 = keep.tile([P, 4 * V], F32, name="picked0", align_bytes=64)
+        picked1 = keep.tile([P, 3 * V + 8 * N + HALF], F32, name="picked1", align_bytes=64)
+        w_raw = [picked1[:, 3 * V + 4 * N * g:3 * V + 4 * N * (g + 1)].rearrange("p (j m) -> p j m", j=4) for g in range(PASSES)]
         w_bf = [[keep.tile([P, N // 2, 4], BF16, name=f"w_bf{g}{h}", tag=f"w_bf{g}{h}", align_bytes=64) for h in range(2)] for g in range(PASSES)]
         w_codes = [keep.tile([P, N], U32, name=f"w_codes{g}", align_bytes=64) for g in range(PASSES)]
         w_scales = [keep.tile([P, N], U8, name=f"w_scales{g}", align_bytes=64) for g in range(PASSES)]
-        x_bf = [keep.tile([P, 4 * V], BF16, name=f"x_bf{g}", align_bytes=64) for g in range(PASSES)]
-        x_codes = [keep.tile([P, V], U32, name=f"x_codes{g}", align_bytes=64) for g in range(PASSES)]
+        x_bf = keep.tile([P, 4 * V], BF16, name="x_bf", align_bytes=64)
+        x_codes = keep.tile([P, V], U32, name="x_codes", align_bytes=64)
         x_scales = [keep.tile([P, V], U8, name=f"x_scales{g}", align_bytes=64) for g in range(PASSES)]
         banks = [psum.tile([P, 512], F32, name=f"bank{i}") for i in range(8)]
         result = [keep.tile([P, BLOCKS, hi - lo], F32, name=f"result{i}") for i, (lo, hi) in enumerate(PIECES)]
@@ -56,19 +55,26 @@ def tile_picked_hash_lin_silu_sub_l_kernel(tc, xT, w, b, offs, out):
                 return d * V + v
             if v < HALF:
                 return 2 * V + d * HALF + v
-            return 3 * V + d * HALF + v - HALF
+            if v < 384:
+                return 3 * V + 8 * N + d * P
+            return 3 * V + 4 * N + d * 256
 
         def sums(g, lo, hi):
-            if g == 1 and hi <= HALF:
-                return w_raw0[:, 2 * lo:2 * hi].bitcast(BF16)
-            return x_bf[g][:, 4 * lo:4 * hi]
+            if g == 0:
+                return x_bf[:, 4 * lo:4 * hi]
+            if lo < 384:
+                return w_raw[0][:, 1 + lo // P, 0:256].bitcast(BF16)
+            return w_raw[1][:, 1, 2 * (lo - HALF):2 * (hi - HALF)].bitcast(BF16)
 
+        early_codes = []
         late_codes = []
 
         def codes(g, lo, hi):
             if g == 0 and lo >= HALF:
                 return late_codes[0][:, lo - HALF:hi - HALF].bitcast(FP8X4)
-            return x_codes[g][:, lo:hi].bitcast(FP8X4)
+            if g == 0:
+                return early_codes[0][:, lo:hi].bitcast(FP8X4)
+            return x_codes[:, lo:hi].bitcast(FP8X4)
 
         def pack(g, u, lo, hi, engine):
             halves = table[g][u][:, 1, :].bitcast(BF16).rearrange("p (t e) -> p t e", e=2)
@@ -101,10 +107,10 @@ def tile_picked_hash_lin_silu_sub_l_kernel(tc, xT, w, b, offs, out):
             nc.vector.tensor_copy(words, window.indirect(offsets[:, (d * V + lo) // 16:(d * V + hi) // 16]))
 
         def pairs(g, d, lo, hi):
-            first = place(g, 0, d, lo)
-            step = place(g, 1, d, lo) - first
-            both = (picked0, picked1)[g][:, first:first + 2 * step].bitcast(BF16).rearrange("p (u v e) -> p v u e", u=2, e=2)
-            return both[:, 0:hi - lo, :, :]
+            n = hi - lo
+            first, second = place(g, 0, d, lo) // n, place(g, 1, d, lo) // n
+            runs = (picked0, picked1)[g][:, :].bitcast(BF16).rearrange("p (r v e) -> p v r e", v=n, e=2)
+            return runs[:, :, first:second + 1:second - first, :]
 
         def add(g, lo, hi, engine=nc.vector):
             engine.tensor_tensor(
@@ -116,8 +122,8 @@ def tile_picked_hash_lin_silu_sub_l_kernel(tc, xT, w, b, offs, out):
 
         def acc(i, c):
             lo, hi = PIECES[i]
-            if i == len(PIECES) - 1:
-                return banks[BLOCKS + c][:, 0:hi - lo]
+            if i > 0 and c >= 2:
+                return banks[2 * i + c][:, 0:hi - lo]
             return banks[c][:, lo:hi]
 
         def multiply(i, c, g):
@@ -160,11 +166,11 @@ def tile_picked_hash_lin_silu_sub_l_kernel(tc, xT, w, b, offs, out):
         pack(0, 1, 0, 400, "v")
         pack(0, 1, 400, T, "s")
         gather(0, 1, 0, 0, V)
-        gather(0, 1, 1, 0, HALF)
-        gather(0, 1, 1, HALF, V)
-        add(0, 0, HALF)
-        add(0, HALF, V)
-        quantise_x(0, 0, HALF)
+        gather(0, 1, 1, 384, V)
+        gather(0, 1, 1, 0, 384)
+        add(0, 384, V)
+        add(0, 0, HALF, nc.gpsimd)
+        add(0, HALF, 384, nc.gpsimd)
         pack(1, 0, 0, T, "s")
         gather(1, 0, 0, 0, V)
         gather(1, 0, 1, 0, V)
@@ -176,37 +182,50 @@ def tile_picked_hash_lin_silu_sub_l_kernel(tc, xT, w, b, offs, out):
         a, m, z = PIECES
         gather(1, 1, 0, *a)
         gather(1, 1, 1, *a)
+        gather(1, 1, 0, *m)
+        gather(1, 1, 1, *m)
         quantise_w(0, 0, 256)
-        add(1, *a)
+        add(1, 0, P)
+        add(1, P, HALF)
+        add(1, *m)
+        early_codes.append(keep.tile([P, HALF], U32, name="early_codes", tag="w_bf00", align_bytes=64))
+        quantise_x(0, 0, HALF)
+        quantise_x(1, 0, P)
+        quantise_x(1, P, HALF)
+        quantise_x(1, *m)
         quantise_w(0, 256, 512)
-        quantise_x(1, *a)
         for c in range(BLOCKS):
             multiply(0, c, 0)
         quantise_w(1, 0, 256)
-        gather(1, 1, 0, *m)
+        gather(1, 1, 0, *z)
         late_codes.append(keep.tile([P, HALF], U32, name="late_codes", tag="w_bf10", align_bytes=64))
         quantise_x(0, HALF, V)
-        gather(1, 1, 0, *z)
-        quantise_w(1, 256, 512)
-        for c in range(BLOCKS):
+        for c in range(2):
             multiply(0, c, 1)
             finish(0, c)
-            if c % 2 == 1:
-                store(0, c - 1, c + 1, nc.sync)
-        for c in range(BLOCKS):
-            multiply(2, c, 0)
-        for c in range(BLOCKS):
+        store(0, 0, 2, nc.sync)
+        for c in range(2):
             multiply(1, c, 0)
-        gather(1, 1, 1, *m)
-        gather(1, 1, 1, *z)
-        add(1, *m)
-        add(1, *z)
-        quantise_x(1, *m)
-        quantise_x(1, *z)
-        for c in range(BLOCKS):
             multiply(1, c, 1)
             finish(1, c)
-        store(1, 0, BLOCKS, nc.sync)
+        store(1, 0, 2, nc.sync)
+        for c in range(2, 4):
+            multiply(1, c, 0)
+            multiply(2, c, 0)
+        for c in range(2):
+            multiply(2, c, 0)
+        quantise_w(1, 256, 512)
+        gather(1, 1, 1, *z)
+        add(1, *z)
+        quantise_x(1, *z)
+        for c in range(2, 4):
+            multiply(0, c, 1)
+            finish(0, c)
+        store(0, 2, 4, nc.sync)
+        for c in range(2, 4):
+            multiply(1, c, 1)
+            finish(1, c)
+        store(1, 2, 4, nc.sync)
         for c in range(BLOCKS):
             multiply(2, c, 1)
             finish(2, c)

from contextlib import ExitStack

import concourse.mybir as mybir

K, T, D, V, N = 1024, 1024, 2, 512, 512
FLOPS = 2 * K * V * N

F32 = mybir.dt.float32
BF16 = mybir.dt.bfloat16
U32 = mybir.dt.uint32
U16 = mybir.dt.uint16
U8 = mybir.dt.uint8
FP8X4 = mybir.dt.float8_e4m3fn_x4
SILU = mybir.ActivationFunctionType.Silu
ADD = mybir.AluOpType.add
MULT = mybir.AluOpType.mult

P = 128
PASSES = 2
BLOCKS = N // P
HALF = V // 2
PIECES = ((0, 256), (256, 384), (384, 512))


def tile_picked_hash_lin_silu_sub_l_kernel(tc, xT, w, b, offs, out):
    nc = tc.nc
    x_rows = xT.rearrange("(g p u e) t -> g u p e t", g=PASSES, p=P, u=2, e=2)
    w_rows = w.rearrange("(g p j) m -> g p j m", g=PASSES, p=P, j=4)
    out_rows = out.rearrange("(c p) v -> p c v", p=P)

    with ExitStack() as ctx:
        keep = ctx.enter_context(tc.tile_pool(name="keep", bufs=1))
        psum = ctx.enter_context(tc.psum_pool(name="psum", bufs=1))

        offsets = keep.tile([P, D * V // 16], U16, name="offsets")
        bias = keep.tile([P, BLOCKS], F32, name="bias")
        table = [[keep.tile([P, 2, T], F32, name=f"table{g}{u}", align_bytes=64) for u in range(2)] for g in range(PASSES)]
        picked0 = keep.tile([P, 4 * V], F32, name="picked0", align_bytes=64)
        picked1 = keep.tile([P, 3 * V + 8 * N + HALF], F32, name="picked1", align_bytes=64)
        w_raw = [picked1[:, 3 * V + 4 * N * g:3 * V + 4 * N * (g + 1)].rearrange("p (j m) -> p j m", j=4) for g in range(PASSES)]
        w_bf = [[keep.tile([P, N // 2, 4], BF16, name=f"w_bf{g}{h}", tag=f"w_bf{g}{h}", align_bytes=64) for h in range(2)] for g in range(PASSES)]
        w_codes = [keep.tile([P, N], U32, name=f"w_codes{g}", align_bytes=64) for g in range(PASSES)]
        w_scales = [keep.tile([P, N], U8, name=f"w_scales{g}", align_bytes=64) for g in range(PASSES)]
        x_bf = keep.tile([P, 4 * V], BF16, name="x_bf", align_bytes=64)
        x_codes = keep.tile([P, V], U32, name="x_codes", align_bytes=64)
        x_scales = [keep.tile([P, V], U8, name=f"x_scales{g}", align_bytes=64) for g in range(PASSES)]
        banks = [psum.tile([P, 512], F32, name=f"bank{i}") for i in range(8)]
        result = [keep.tile([P, BLOCKS, hi - lo], F32, name=f"result{i}") for i, (lo, hi) in enumerate(PIECES)]
        warm = keep.tile([P, 2], F32, name="warm")

        def place(g, u, d, v):
            if g == 0:
                return (2 * d + u) * V + v
            if u == 0:
                return d * V + v
            if v < HALF:
                return 2 * V + d * HALF + v
            if v < 384:
                return 3 * V + 8 * N + d * P
            return 3 * V + 4 * N + d * 256

        def sums(g, lo, hi):
            if g == 0:
                return x_bf[:, 4 * lo:4 * hi]
            if lo < 384:
                return w_raw[0][:, 1 + lo // P, 0:256].bitcast(BF16)
            return w_raw[1][:, 1, 2 * (lo - HALF):2 * (hi - HALF)].bitcast(BF16)

        early_codes = []
        late_codes = []

        def codes(g, lo, hi):
            if g == 0 and lo >= HALF:
                return late_codes[0][:, lo - HALF:hi - HALF].bitcast(FP8X4)
            if g == 0:
                return early_codes[0][:, lo:hi].bitcast(FP8X4)
            return x_codes[:, lo:hi].bitcast(FP8X4)

        def pack(g, u, lo, hi, engine):
            halves = table[g][u][:, 1, :].bitcast(BF16).rearrange("p (t e) -> p t e", e=2)
            if engine == "v":
                nc.vector.tensor_copy(out=halves[:, lo:hi, 0], in_=table[g][u][:, 0, lo:hi])
            elif engine == "g":
                nc.gpsimd.tensor_copy(out=halves[:, lo:hi, 0], in_=table[g][u][:, 0, lo:hi])
            else:
                nc.scalar.copy(out=halves[:, lo:hi, 0], in_=table[g][u][:, 0, lo:hi])

        def weave_w(g, lo, hi):
            dst = w_bf[g][lo // 256][:, :, :].rearrange("p (c i) j -> p c j i", i=4)
            src = w_raw[g][:, :, lo:hi].rearrange("p j (c i) -> p c j i", i=4)
            nc.scalar.copy(out=dst, in_=src)

        def quantise_w(g, lo, hi):
            nc.vector.quantize_mx(
                out=w_codes[g][:, lo:hi].bitcast(FP8X4),
                scales=w_scales[g][:, lo:hi],
                in_=w_bf[g][lo // 256][:, :, :].rearrange("p n j -> p (n j)"),
            )

        def quantise_x(g, lo, hi):
            nc.vector.quantize_mx(out=codes(g, lo, hi), scales=x_scales[g][:, lo:hi], in_=sums(g, lo, hi))

        def gather(g, u, d, lo, hi):
            window = table[g][u][:, 1, :].bitcast(U32)
            first = place(g, u, d, lo)
            words = (picked0, picked1)[g][:, first:first + hi - lo].bitcast(U32)
            nc.vector.tensor_copy(words, window.indirect(offsets[:, (d * V + lo) // 16:(d * V + hi) // 16]))

        def pairs(g, d, lo, hi):
            n = hi - lo
            first, second = place(g, 0, d, lo) // n, place(g, 1, d, lo) // n
            runs = (picked0, picked1)[g][:, :].bitcast(BF16).rearrange("p (r v e) -> p v r e", v=n, e=2)
            return runs[:, :, first:second + 1:second - first, :]

        def add(g, lo, hi, engine=nc.vector):
            engine.tensor_tensor(
                out=sums(g, lo, hi).rearrange("p (v u e) -> p v u e", u=2, e=2),
                in0=pairs(g, 0, lo, hi),
                in1=pairs(g, 1, lo, hi),
                op=ADD,
            )

        def acc(i, c):
            lo, hi = PIECES[i]
            if i > 0 and c >= 2:
                return banks[2 * i + c][:, 0:hi - lo]
            return banks[c][:, lo:hi]

        def multiply(i, c, g):
            lo, hi = PIECES[i]
            cols = slice(c * P, (c + 1) * P)
            nc.tensor.matmul_mx(
                out=acc(i, c),
                lhsT=w_codes[g][:, cols].bitcast(FP8X4),
                lhsT_scale=w_scales[g][:, cols],
                rhs=codes(g, lo, hi),
                rhs_scale=x_scales[g][:, lo:hi],
                start=(g == 0),
                stop=(g == PASSES - 1),
            )

        def finish(i, c):
            nc.scalar.activation(out=result[i][:, c, :], in_=acc(i, c), func=SILU, bias=bias[:, c:c + 1])

        def store(i, c0, c1, queue):
            lo, hi = PIECES[i]
            queue.dma_start(out=out_rows[:, c0:c1, lo:hi], in_=result[i][:, c0:c1, :])

        nc.vector.memset(warm[:, 0:1], 0.0)
        nc.scalar.activation(out=warm[:, 1:2], in_=warm[:, 0:1], func=SILU)

        nc.sync.dma_start(out=table[0][0][:], in_=x_rows[0, 0])
        nc.sync.dma_start(offsets[:], offs)
        nc.sync.dma_start(out=table[0][1][:], in_=x_rows[0, 1])
        nc.sync.dma_start(out=table[1][0][:], in_=x_rows[1, 0])
        nc.sync.dma_start(out=table[1][1][:], in_=x_rows[1, 1])
        nc.sync.dma_start(out=w_raw[0], in_=w_rows[0])
        nc.sync.dma_start(out=w_raw[1], in_=w_rows[1])
        with nc.allow_non_contiguous_dma(reason="one bias value a partition and block"):
            nc.sync.dma_start(out=bias[:], in_=b.rearrange("(c p) o -> p (c o)", p=P))

        pack(0, 0, 0, 688, "v")
        pack(0, 0, 688, T, "s")
        gather(0, 0, 0, 0, V)
        gather(0, 0, 1, 0, V)
        pack(0, 1, 0, 400, "v")
        pack(0, 1, 400, T, "s")
        gather(0, 1, 0, 0, V)
        gather(0, 1, 1, 384, V)
        gather(0, 1, 1, 0, 384)
        add(0, 384, V)
        add(0, 0, HALF, nc.gpsimd)
        add(0, HALF, 384, nc.gpsimd)
        pack(1, 0, 0, T, "s")
        gather(1, 0, 0, 0, V)
        gather(1, 0, 1, 0, V)
        pack(1, 1, 0, T, "s")
        weave_w(0, 0, 256)
        weave_w(0, 256, 512)
        weave_w(1, 0, 256)
        weave_w(1, 256, 512)
        a, m, z = PIECES
        gather(1, 1, 0, *a)
        gather(1, 1, 1, *a)
        gather(1, 1, 0, *m)
        gather(1, 1, 1, *m)
        quantise_w(0, 0, 256)
        add(1, 0, P)
        add(1, P, HALF)
        add(1, *m)
        early_codes.append(keep.tile([P, HALF], U32, name="early_codes", tag="w_bf00", align_bytes=64))
        quantise_x(0, 0, HALF)
        quantise_x(1, 0, P)
        quantise_x(1, P, HALF)
        quantise_x(1, *m)
        quantise_w(0, 256, 512)
        for c in range(BLOCKS):
            multiply(0, c, 0)
        quantise_w(1, 0, 256)
        gather(1, 1, 0, *z)
        late_codes.append(keep.tile([P, HALF], U32, name="late_codes", tag="w_bf10", align_bytes=64))
        quantise_x(0, HALF, V)
        for c in range(2):
            multiply(0, c, 1)
            finish(0, c)
        store(0, 0, 2, nc.sync)
        for c in range(2):
            multiply(1, c, 0)
            multiply(1, c, 1)
            finish(1, c)
        store(1, 0, 2, nc.sync)
        for c in range(2, 4):
            multiply(1, c, 0)
            multiply(2, c, 0)
        for c in range(2):
            multiply(2, c, 0)
        quantise_w(1, 256, 512)
        gather(1, 1, 1, *z)
        add(1, *z)
        quantise_x(1, *z)
        for c in range(2, 4):
            multiply(0, c, 1)
            finish(0, c)
        store(0, 2, 4, nc.sync)
        for c in range(2, 4):
            multiply(1, c, 1)
            finish(1, c)
        store(1, 2, 4, nc.sync)
        for c in range(BLOCKS):
            multiply(2, c, 1)
            finish(2, c)
            if c == 1:
                store(2, 0, 2, nc.sync)
            if c == 2:
                store(2, 2, 3, nc.sync)
        store(2, 3, 4, nc.scalar)
